import numpy as np, ml_dtypes
CORES = [16,32,48,64,80]
N = 5
BF = ml_dtypes.bfloat16
def gentries(a):
    return np.ascontiguousarray(a.reshape(8, 16, -1).transpose(0, 2, 1)).reshape(8, -1)
def gtable(e):
    e = np.asarray(e); return np.ascontiguousarray(e.reshape(8, -1, 16).transpose(0, 2, 1)).reshape(128, -1).astype(np.int32)
def f(rng, *shape):
    return (rng.standard_normal(shape, dtype=np.float32) * np.exp2(rng.integers(-2, 3, shape[:-1] + (1,)))).astype(BF)
def wide(rng, *shape):
    v = f(rng, *shape).astype(np.float32); k = shape[:-2] + (1, shape[-1])
    return (v * np.exp2(rng.integers(-6, 7, k)) * (rng.random(k) > 0.0625)).astype(BF)
P, E, M, G = 3072, 8192, 128, 32
Z = P + (N - 1) * G
DX, DY = (-1, 0, 1, -1, 1, -1, 0, 1), (-1, -1, -1, 0, 0, 1, 1, 1)
FAR = [[(d, s) for d in range(8) for s in range(4) if max(abs(2 * DX[d] + s % 2 - c % 2), abs(2 * DY[d] + s // 2 - c // 2)) > 1] for c in range(4)]
def kids(rng):
    return rng.permuted(np.tile(np.minimum(np.arange(4 * P), E), (N, 8, 1)), axis=2).reshape(N, 8, 4, P)
def nears(rng, own, ghost):
    u = rng.random((N, 8, 8, M))
    return np.where(u < own, rng.integers(0, P, u.shape), np.where(u < own + ghost, rng.integers(P, Z, u.shape), Z))
def gives(rng):
    return rng.integers(0, P, (N, 8, N - 1, G))
def pack(rng, ki, ne, gi):
    return {"ex": f(rng, N, 128, E), "kid": ki.reshape(N, 8, 4 * P).astype(np.int32), "near": np.stack([gtable(a.reshape(8, 8 * M)) for a in ne]),
            "give": np.stack([gtable(a.reshape(8, (N - 1) * G)) for a in gi]), "tr": f(rng, N, 128, 108)}
def setup_inputs(rng):
    return pack(rng, kids(rng), nears(rng, 0.5, 0.42), gives(rng))
def setup_inputs_ghosts(rng):
    ne = nears(rng, 0.0, 2.0); q = rng.integers(0, N); ne[q] = P + G * rng.integers(0, N - 1) + rng.integers(0, G, (8, 8, M))
    for b in range(N - 1):
        ne[:, :, b, 0] = P + G * b; ne[:, :, b, M - 1] = P + G * b + G - 1
    return pack(rng, kids(rng), ne, gives(rng))
def setup_inputs_empty(rng):
    ne = nears(rng, 0.15, 0.15); ne[:, :, :, ::4] = Z; ne[:, rng.choice(np.array([0, 3, 4, 6, 7]))] = Z
    ki = kids(rng); ki[:, :, :, rng.random(P) < 0.5] = E; b = rng.integers(0, P)
    ki[:, :, :, b] = rng.integers(0, E, (N, 8, 4)); ne[:, 1:3, 0, 1] = b
    ne[:, 5, 7, 2] = b
    return pack(rng, ki, ne, gives(rng))
def setup_inputs_ends(rng):
    ne = rng.choice(np.array([0, P - 1, P, P + G - 1, Z - G, Z - 1, Z]), (N, 8, 8, M)); ki = kids(rng)
    for p in (0, P - 1): ki[:, :, :, p] = rng.permuted(np.tile(np.array([0, E - 1, E, E - 1]), (N, 8, 1)), axis=2)
    return pack(rng, ki, ne, rng.choice(np.array([0, P - 1]), (N, 8, N - 1, G)))
def setup_inputs_alike(rng):
    ne = np.tile(rng.integers(0, Z, (N, 8, 8, 1)), (1, 1, 1, M)); gi = np.tile(rng.integers(0, P, (N, 8, N - 1, 1)), (1, 1, 1, G))
    return pack(rng, rng.integers(0, E, (N, 8, 4, P)), ne, gi)
def setup_inputs_spread(rng):
    d = setup_inputs(rng); d["ex"] = wide(rng, N, 128, E); return d
def check_inputs(d):
    bad = []
    for a, top in (("kid", E), ("near", Z), ("give", P - 1)):
        if d[a].min() < 0 or d[a].max() > top: bad.append(a)
    for a in ("ex", "tr"):
        if not np.isfinite(d[a].astype(np.float32)).all(): bad.append(a)
    return bad
def reference(ex, kid, near, give, tr):
    x = np.concatenate([ex.astype(np.float64).reshape(N, 8, 16, E), np.zeros((N, 8, 16, 1))], 3)
    ch = kid.reshape(N, 8, 4, P); t = tr.astype(np.float64).reshape(N, 8, 16, 4, 27)
    gi = [gentries(a).reshape(8, N - 1, G) for a in give]; ne = [gentries(a).reshape(8, 8, M) for a in near]
    y = np.zeros((N, 8, 16, 4, M), np.float64)
    for r in range(N):
        for g in range(8):
            w = [x[r, g][:, ch[r, g]]]
            for d in range(1, N):
                q = (r - d) % N
                w.append(x[q, g][:, ch[q, g][:, gi[q][g, d - 1]]])
            w = np.concatenate(w + [np.zeros((16, 4, 1))], 2)
            v = w[:, :, ne[r][g]]
            for c in range(4):
                for i, (d, s) in enumerate(FAR[c]):
                    y[r, g, :, c] += t[r, g, :, c, i, None] * v[:, s, d]
    return {"y": y.reshape(N, 128, 4 * M).astype(np.float32)}

@@ -1,0 +1,303 @@
+from concourse.bass import DstId, RemoteDMATransfer
+from concourse.mybir import AluOpType, ActivationFunctionType
+
+N, P, E, M, G = 5, 3072, 8192, 128, 32
+DX, DY = (-1, 0, 1, -1, 1, -1, 0, 1), (-1, -1, -1, 0, 0, 1, 1, 1)
+HALF = E // 2
+D0 = 16
+Z1 = D0 + HALF
+G0 = Z1 + 16
+WW = G0 + 4 * G * (N - 1)
+KQ = P // 4
+KV = 22
+
+SCRATCH = {
+    "win0": ("sbuf", [128, WW], "bfloat16"),
+    "win1": ("sbuf", [128, WW], "bfloat16"),
+    "kt": ("sbuf", [128, KQ + 136], "int32"),
+    "ng": ("sbuf", [128, 72], "int32"),
+    "t1": ("sbuf", [128, 72], "int32"),
+    "t2": ("sbuf", [128, 72], "int32"),
+    "t3": ("sbuf", [128, 72], "int32"),
+    "clsu": ("sbuf", [128, 72], "uint16"),
+    "colu": ("sbuf", [128, 72], "uint16"),
+    "trs": ("sbuf", [128, 108], "bfloat16"),
+    "trb": ("sbuf", [128, 256], "bfloat16"),
+    "pi": ("sbuf", [128, 8], "int32"),
+    "pf": ("sbuf", [128, 16], "float32"),
+    "r1": ("sbuf", [128, 128], "float32"),
+    "prm": ("sbuf", [128, 256], "bfloat16"),
+    "sel": ("sbuf", [128, 1024], "float32"),
+    "mt": ("sbuf", [128, 8], "float32"),
+    "dmb": ("sbuf", [128, 32], "bfloat16"),
+    "dmf": ("sbuf", [128, 32], "float32"),
+    "msk": ("sbuf", [128, 1152], "float32"),
+    "l1": ("sbuf", [128, 1152], "float32"),
+    "gx": ("sbuf", [128, 64], "float32"),
+    "goff": ("sbuf", [128, 64], "uint16"),
+    "nx": ("sbuf", [128, 512], "float32"),
+    "noff": ("sbuf", [128, 512], "uint16"),
+    "wt": ("sbuf", [128, 8192], "bfloat16"),
+    "gs": ("sbuf", [128, 1024], "bfloat16"),
+    "vv": ("sbuf", [128, 8192], "bfloat16"),
+    "ys": ("sbuf", [128, 512], "float32"),
+    "pg0": ("psum", [128, 512], "float32"),
+    "pg1": ("psum", [128, 512], "float32"),
+    "pn0": ("psum", [128, 512], "float32"),
+    "pn1": ("psum", [128, 512], "float32"),
+    "py0": ("psum", [128, 512], "float32"),
+    "py1": ("psum", [128, 512], "float32"),
+    "py2": ("psum", [128, 512], "float32"),
+    "py3": ("psum", [128, 512], "float32"),
+}
+SEMAPHORES = ["sv", "sa", "sp", "sg", "lng", "ltr", "lkid", "lex0", "lex1", "arr0", "arr1", "sent", "st0", "st1"]
+
+
+def far_runs():
+    runs = []
+    for c in range(4):
+        i = 0
+        last = -2
+        for ds in range(32):
+            d, s = divmod(ds, 4)
+            if max(abs(2 * DX[d] + s % 2 - c % 2), abs(2 * DY[d] + s // 2 - c // 2)) > 1:
+                if ds == last + 1:
+                    runs[-1][3] += 1
+                else:
+                    runs.append([c, ds, 27 * c + i, 1])
+                last = ds
+                i += 1
+    return runs
+
+
+def rank_program(g, core, T, topo):
+    rank = T.rank_of(core)
+    if rank is None:
+        return
+    A = AluOpType
+    COPY = ActivationFunctionType.Copy
+    IDENT = ActivationFunctionType.Identity
+    queue = {"v": g.vector, "a": g.scalar, "p": g.tensor, "g": g, "s": g.sync}
+    counter = {"v": "sv", "a": "sa", "p": "sp", "g": "sg"}
+    count = {"v": 0, "a": 0, "p": 0, "g": 0}
+    seen = {}
+
+    def wait(q, *deps):
+        for name, val in deps:
+            if seen.get((q, name), 0) < val:
+                queue[q].wait_ge(T.sem[name], val)
+                seen[(q, name)] = val
+
+    def done(q, ins):
+        ins.then_inc(T.sem[counter[q]], 1)
+        count[q] += 1
+        return (counter[q], count[q])
+
+    V, S, PE = g.vector, g.scalar, g.tensor
+    win = [T.win0, T.win1]
+    pg, pn, py = [T.pg0, T.pg1], [T.pn0, T.pn1], [T.py0, T.py1, T.py2, T.py3]
+    ptr = T.py3
+
+    S.dma_start(T.ng[:, 0:8], T.give[:]).then_inc(T.sem.lng, 16)
+    S.dma_start(T.ng[:, 8:72], T.near[:]).then_inc(T.sem.lng, 16)
+    S.dma_start(T.trs[:], T.tr[:]).then_inc(T.sem.ltr, 16)
+    g.sync.dma_start(T.kt[:, 0:KQ], T.kid[:]).then_inc(T.sem.lkid, 16)
+    for X in range(2):
+        for Q in range(2):
+            for h in range(2):
+                p0, r0 = 64 * Q + 32 * h, 64 * X + 32 * Q
+                g.sync.dma_start(win[X][p0:p0 + 32, D0:Z1],
+                                 T.ex[r0:r0 + 32, HALF * h:HALF * (h + 1)]).then_inc(T.sem["lex%d" % X], 16)
+    LEX = [("lex0", 64), ("lex1", 64)]
+
+    i_p = done("g", g.iota(T.pi[:, 0:1], [[0, 1]], 0, 1))
+    i_r = done("g", g.iota(T.r1[:], [[32, 2], [0, 2], [1, 32]], 0, 0, allow_small_or_imprecise_dtypes=True))
+    i_k = done("g", g.iota(T.kt[:, KQ:KQ + 128], [[4, 128]], E + 20, 0))
+
+    done("v", V.memset(ptr[:, 0:256], 0.0))
+    done("v", V.memset(T.kt[:, KQ + 128:KQ + 136], E))
+    for X in range(2):
+        done("v", V.memset(win[X][:, 0:D0], 0.0))
+        done("v", V.memset(win[X][:, Z1:G0], 0.0))
+    wait("v", i_p)
+    p = T.pi[:, 0:1]
+    done("v", V.tensor_scalar(T.pi[:, 1:2], p, 31, None, A.bitwise_and))
+    done("v", V.tensor_scalar(T.pi[:, 2:3], p, 3, None, A.bitwise_and))
+    done("v", V.tensor_scalar(T.pi[:, 3:4], p, 112, None, A.bitwise_and))
+    done("v", V.tensor_scalar(T.pi[:, 4:5], p, 2, 3, A.arith_shift_right, A.bitwise_and))
+    x = done("v", V.tensor_scalar(T.pi[:, 5:6], p, 5, 1, A.arith_shift_right, A.bitwise_and))
+    wait("v", x)
+    x = done("v", V.tensor_copy(T.pf[:, 0:6], T.pi[:, 0:6]))
+    wait("v", x, i_r)
+    f_p, f_k, f_lo, f_code, f_c, f_a1, f_a2 = (T.pf[:, j:j + 1] for j in (0, 1, 2, 6, 7, 8, 9))
+    c_code = done("v", V.tensor_scalar(f_code, T.pf[:, 3:4], T.pf[:, 4:5], None, A.add))
+    c_c = done("v", V.tensor_scalar(f_c, T.pf[:, 5:6], float(-HALF), float(D0), A.mult, A.add))
+    done("v", V.tensor_scalar(f_a2, T.pf[:, 5:6], float(HALF), float(Z1 - D0), A.mult, A.add))
+    for X in range(2):
+        c_perm = done("v", V.tensor_scalar(T.prm[:, 128 * X:128 * X + 128], T.r1[:], float(64 * X), f_p,
+                                           A.add, A.is_equal))
+    done("v", V.tensor_scalar(T.mt[:], T.r1[:, 0:8], f_lo, None, A.is_equal))
+    wait("v", c_code, c_c)
+    done("v", V.tensor_scalar(f_a1, f_c, float(E + 20 - G0), f_lo, A.add, A.subtract))
+
+    def make_sel(X):
+        for r in range(4):
+            o = 128 * (4 * X + r)
+            x = done("v", V.tensor_scalar(T.sel[:, o:o + 128], T.r1[:], float(64 * X - 4 * r), f_code,
+                                          A.add, A.is_equal))
+        return x
+
+    c_sel0 = make_sel(0)
+
+    wait("p", c_perm, ("ltr", 16))
+    for X in range(2):
+        for c, ds, col, n in far_runs():
+            o = 64 * c + 32 * X + ds
+            m_tr = done("p", PE.matmul(ptr[:, o:o + n], T.prm[:, 128 * X:128 * X + 128],
+                                       T.trs[:, col:col + n], True, True))
+
+    wait("v", ("lng", 32))
+    x = done("v", V.tensor_scalar(T.t1[:], T.ng[:], float(3 * KQ), 2731.0, A.min, A.mult))
+    wait("v", x)
+    x = done("v", V.tensor_scalar(T.t2[:], T.t1[:], 21, None, A.arith_shift_right))
+    wait("v", x)
+    c_cls = done("v", V.tensor_copy(T.clsu[:], T.t2[:]))
+    x = done("v", V.tensor_scalar(T.t3[:], T.t2[:], float(-KQ), None, A.mult))
+    wait("v", x)
+    x = done("v", V.tensor_tensor(T.t1[:], T.t3[:], T.ng[:], A.add))
+    wait("v", x)
+    c_col = done("v", V.tensor_copy(T.colu[:], T.t1[:]))
+    c_sel1 = make_sel(1)
+
+    wait("a", c_cls)
+    a_m = []
+    for c0, c1 in ((0, 8), (8, 40), (40, 72)):
+        a_m.append(done("a", S.activation(T.msk[:, 16 * c0:16 * c1], T.mt[:].indirect(T.clsu[:, c0:c1]), COPY)))
+    wait("a", m_tr)
+    a_tr = done("a", S.activation(T.trb[:], ptr[:, 0:256], COPY))
+
+    def children(k, c0, c1):
+        wait("v", a_m[k])
+        return done("v", V.tensor_tensor(T.l1[:, 16 * c0:16 * c1], T.kt[:].indirect(T.colu[:, c0:c1]),
+                                         T.msk[:, 16 * c0:16 * c1], A.mult))
+
+    def to_lists(out, X, c0, c1):
+        for r in range(4):
+            o = 128 * (4 * X + r)
+            ins = PE.matmul(out, T.sel[:, o:o + 128], T.l1[:, c0 + r:c1:4], r == 0, r == 3)
+        return done("p", ins)
+
+    wait("v", c_col, ("lkid", 16), i_k)
+    v_g = children(0, 0, 8)
+    v_n0 = children(1, 8, 40)
+    wait("p", v_g, c_sel0, c_sel1)
+    m_g = [to_lists(pg[X][:, 0:32], X, 0, 128) for X in range(2)]
+    c_goff = []
+    for X in range(2):
+        wait("v", m_g[X])
+        x = done("v", V.tensor_scalar(T.gx[:, 32 * X:32 * X + 32], pg[X][:, 0:32], f_c, 0.0, A.add, A.max))
+        wait("v", x)
+        c_goff.append(done("v", V.tensor_scalar(T.goff[:, 32 * X:32 * X + 32], T.gx[:, 32 * X:32 * X + 32],
+                                                float(Z1), None, A.min)))
+    done("v", V.tensor_scalar(T.dmb[:, 0:KV], T.r1[:, 0:KV], f_k, None, A.is_equal))
+    c_dm = done("v", V.tensor_scalar(T.dmf[:, KV:32], T.r1[:, KV:32], f_k, None, A.is_equal))
+    v_n1 = children(2, 40, 72)
+    m_n = []
+    for X in range(2):
+        wait("p", v_n0)
+        to_lists(pn[X][:, 0:128], X, 128, 640)
+        wait("p", v_n1)
+        m_n.append(to_lists(pn[X][:, 128:256], X, 640, 1152))
+
+    def gather(q, out, window, offs):
+        if q == "v":
+            return done("v", V.tensor_copy(out, window.indirect(offs)))
+        return done("a", S.activation(out, window.indirect(offs), COPY))
+
+    peers = [T.cores[(rank + d) % N] for d in range(1, N)]
+
+    def give_away(X):
+        got = []
+        for k, q in enumerate("va"):
+            wait(q, c_goff[X], LEX[X])
+            o, c = 512 * X + 256 * k, 32 * X + 16 * k
+            got.append(gather(q, T.gs[:, o:o + 256], win[X][:, 0:G0], T.goff[:, c:c + 16]))
+        wait("g", *got)
+        moves = []
+        for k, peer in enumerate(peers):
+            eng = topo.engines(core, peer)
+            per = len(eng) // len(peers)
+            rid, pid = topo.addr(peer)[:2]
+            moves.append(RemoteDMATransfer(
+                dst_ids=[DstId(rid=rid, pnc=pid)], dma_engine_mask=sum(1 << e for e in eng[per * k:per * (k + 1)]),
+                remote_sem=T.sem["arr%d" % X], src=T.gs[:, 512 * X + 128 * k:512 * X + 128 * (k + 1)],
+                dst=win[X][:, G0 + 128 * k:G0 + 128 * (k + 1)]))
+        g.remote_dma_fused(moves, local_sem=T.sem.sent)
+
+    sent = sum(len(topo.engines(core, peer)) // len(peers) for peer in peers)
+    arrive = sum(len(topo.engines(peer, core)) // len(peers) for peer in peers)
+
+    def offsets(X):
+        k, u = pn[X][:, 0:256], T.nx[:, 256 * X:256 * X + 256]
+        wait("v", m_n[X])
+        x = done("v", V.tensor_scalar(u, k, f_a1, f_a2, A.subtract, A.max))
+        wait("v", x)
+        x = done("v", V.tensor_tensor(u, u, k, A.min))
+        wait("v", x)
+        return done("v", V.tensor_scalar(T.noff[:, 256 * X:256 * X + 256], u, f_c, 0.0, A.add, A.max))
+
+    def weights_v(k0, k1):
+        for k in range(k0, k1):
+            x = done("v", V.tensor_scalar(T.wt[:, 256 * k:256 * k + 256], T.trb[:], T.dmb[:, k:k + 1], None, A.mult))
+        return x
+
+    give_away(0)
+    wait("v", a_tr, c_dm)
+    wait("a", a_tr, c_dm)
+    weights_v(0, 12)
+    c_noff = [offsets(0)]
+    w_v = weights_v(12, KV)
+    for k in range(KV, 32):
+        w_a = done("a", S.activation(T.wt[:, 256 * k:256 * k + 256], T.trb[:], IDENT, scale=T.dmf[:, k:k + 1]))
+    give_away(1)
+    c_noff.append(offsets(1))
+
+    wait("p", w_v, w_a)
+    last = {}
+
+    def put_out(X):
+        e = []
+        for Q, q in enumerate("va"):
+            o = 256 * X + 128 * Q
+            wait(q, last[(X, Q)])
+            if q == "v":
+                e.append(done("v", V.tensor_copy(T.ys[:, o:o + 128], py[2 * X + Q][:, 0:128])))
+            else:
+                e.append(done("a", S.activation(T.ys[:, o:o + 128], py[2 * X + Q][:, 0:128], COPY)))
+        for Q in range(2):
+            o, r0 = 256 * X + 128 * Q, 64 * X + 32 * Q
+            q, sem = ("a", T.sem.st1) if (X, Q) == (1, 1) else ("s", T.sem.st0)
+            wait(q, e[Q])
+            queue[q].dma_start(T.y[r0:r0 + 32, :], T.ys[:, o:o + 128]).then_inc(sem, 16)
+
+    for X in range(2):
+        for d in range(8):
+            got = []
+            for k, q in enumerate("va"):
+                wait(q, c_noff[X], ("arr%d" % X, arrive))
+                o, c = 4096 * X + 512 * d + 256 * k, 256 * X + 32 * d + 16 * k
+                got.append(gather(q, T.vv[:, o:o + 256], win[X][:], T.noff[:, c:c + 16]))
+            if X == 1 and d == 0:
+                put_out(0)
+            wait("p", *got)
+            for Q in range(2):
+                for s in range(4):
+                    o = 4096 * X + 512 * d
+                    ins = PE.matmul(py[2 * X + Q][:, 0:128], T.wt[64 * Q:64 * Q + 64, 32 * X + 4 * d + s:8192:64],
+                                    T.vv[64 * Q:64 * Q + 64, o + s:o + 512:4], d == 0 and s == 0, d == 7 and s == 3)
+                if d == 7:
+                    last[(X, Q)] = done("p", ins)
+    put_out(1)
+    wait("s", ("st0", 48))
+    wait("a", ("st1", 16))
+    wait("g", ("sent", 2 * sent))

@@ -9,47 +9,16 @@ Z1 = D0 + HALF
 G0 = Z1 + 16
 WW = G0 + 4 * G * (N - 1)
 KQ = P // 4
-KV = 22
-
-SCRATCH = {
-    "win0": ("sbuf", [128, WW], "bfloat16"),
-    "win1": ("sbuf", [128, WW], "bfloat16"),
-    "kt": ("sbuf", [128, KQ + 136], "int32"),
-    "ng": ("sbuf", [128, 72], "int32"),
-    "t1": ("sbuf", [128, 72], "int32"),
-    "t2": ("sbuf", [128, 72], "int32"),
-    "t3": ("sbuf", [128, 72], "int32"),
-    "clsu": ("sbuf", [128, 72], "uint16"),
-    "colu": ("sbuf", [128, 72], "uint16"),
-    "trs": ("sbuf", [128, 108], "bfloat16"),
-    "trb": ("sbuf", [128, 256], "bfloat16"),
-    "pi": ("sbuf", [128, 8], "int32"),
-    "pf": ("sbuf", [128, 16], "float32"),
-    "r1": ("sbuf", [128, 128], "float32"),
-    "prm": ("sbuf", [128, 256], "bfloat16"),
-    "sel": ("sbuf", [128, 1024], "float32"),
-    "mt": ("sbuf", [128, 8], "float32"),
-    "dmb": ("sbuf", [128, 32], "bfloat16"),
-    "dmf": ("sbuf", [128, 32], "float32"),
-    "msk": ("sbuf", [128, 1152], "float32"),
-    "l1": ("sbuf", [128, 1152], "float32"),
-    "gx": ("sbuf", [128, 64], "float32"),
-    "goff": ("sbuf", [128, 64], "uint16"),
-    "nx": ("sbuf", [128, 512], "float32"),
-    "noff": ("sbuf", [128, 512], "uint16"),
-    "wt": ("sbuf", [128, 8192], "bfloat16"),
-    "gs": ("sbuf", [128, 1024], "bfloat16"),
-    "vv": ("sbuf", [128, 8192], "bfloat16"),
-    "ys": ("sbuf", [128, 512], "float32"),
-    "pg0": ("psum", [128, 512], "float32"),
-    "pg1": ("psum", [128, 512], "float32"),
-    "pn0": ("psum", [128, 512], "float32"),
-    "pn1": ("psum", [128, 512], "float32"),
-    "py0": ("psum", [128, 512], "float32"),
-    "py1": ("psum", [128, 512], "float32"),
-    "py2": ("psum", [128, 512], "float32"),
-    "py3": ("psum", [128, 512], "float32"),
-}
+KV = 23
+SHARE = (("va", "va", "va", "aa", "va", "va", "va", "va"), ("va",) * 8)
+B, F, I, U = "bfloat16", "float32", "int32", "uint16"
+SCRATCH = {n: ("sbuf", [128, w], t) for n, w, t in (
+    ("win0", WW, B), ("win1", WW, B), ("kt", KQ + 136, I), ("ng", 72, I), ("t1", 72, I), ("t2", 72, I),
+    ("t3", 72, I), ("clsu", 72, U), ("colu", 72, U), ("trs", 108, B), ("trb", 256, B), ("pi", 8, I), ("pf", 16, F),
+    ("r1", 128, F), ("prm", 256, B), ("sel", 1024, F), ("mt", 8, F), ("dmb", 32, B), ("dmf", 32, F),
+    ("msk", 1152, F), ("l1", 1152, F), ("gx", 64, F), ("goff", 64, U), ("nx", 512, F), ("noff", 512, U),
+    ("wt", 8192, B), ("gs", 1024, B), ("vv", 8192, B), ("ys", 512, F))}
+SCRATCH.update({n: ("psum", [128, 512], F) for n in ("pg0", "pg1", "pn0", "pn1", "py0", "py1", "py2", "py3")})
 SEMAPHORES = ["sv", "sa", "sp", "sg", "lng", "ltr", "lkid", "lex0", "lex1", "arr0", "arr1", "sent", "st0", "st1"]
 
 
@@ -99,7 +68,7 @@ def rank_program(g, core, T, topo):
     ptr = T.py3
 
     S.dma_start(T.ng[:, 0:8], T.give[:]).then_inc(T.sem.lng, 16)
-    S.dma_start(T.ng[:, 8:72], T.near[:]).then_inc(T.sem.lng, 16)
+    g.sync.dma_start(T.ng[:, 8:72], T.near[:]).then_inc(T.sem.lng, 16)
     S.dma_start(T.trs[:], T.tr[:]).then_inc(T.sem.ltr, 16)
     g.sync.dma_start(T.kt[:, 0:KQ], T.kid[:]).then_inc(T.sem.lkid, 16)
     for X in range(2):
@@ -130,13 +99,15 @@ def rank_program(g, core, T, topo):
     x = done("v", V.tensor_copy(T.pf[:, 0:6], T.pi[:, 0:6]))
     wait("v", x, i_r)
     f_p, f_k, f_lo, f_code, f_c, f_a1, f_a2 = (T.pf[:, j:j + 1] for j in (0, 1, 2, 6, 7, 8, 9))
-    c_code = done("v", V.tensor_scalar(f_code, T.pf[:, 3:4], T.pf[:, 4:5], None, A.add))
-    c_c = done("v", V.tensor_scalar(f_c, T.pf[:, 5:6], float(-HALF), float(D0), A.mult, A.add))
-    done("v", V.tensor_scalar(f_a2, T.pf[:, 5:6], float(HALF), float(Z1 - D0), A.mult, A.add))
     for X in range(2):
         c_perm = done("v", V.tensor_scalar(T.prm[:, 128 * X:128 * X + 128], T.r1[:], float(64 * X), f_p,
                                            A.add, A.is_equal))
+    c_code = done("v", V.tensor_scalar(f_code, T.pf[:, 3:4], T.pf[:, 4:5], None, A.add))
+    c_c = done("v", V.tensor_scalar(f_c, T.pf[:, 5:6], float(-HALF), float(D0), A.mult, A.add))
+    done("v", V.tensor_scalar(f_a2, T.pf[:, 5:6], float(HALF), float(Z1 - D0), A.mult, A.add))
     done("v", V.tensor_scalar(T.mt[:], T.r1[:, 0:8], f_lo, None, A.is_equal))
+    done("v", V.tensor_scalar(T.dmb[:, 0:KV], T.r1[:, 0:KV], f_k, None, A.is_equal))
+    c_dm = done("v", V.tensor_scalar(T.dmf[:, KV:32], T.r1[:, KV:32], f_k, None, A.is_equal))
     wait("v", c_code, c_c)
     done("v", V.tensor_scalar(f_a1, f_c, float(E + 20 - G0), f_lo, A.add, A.subtract))
 
@@ -169,15 +140,11 @@ def rank_program(g, core, T, topo):
     c_col = done("v", V.tensor_copy(T.colu[:], T.t1[:]))
     c_sel1 = make_sel(1)
 
-    wait("a", c_cls)
-    a_m = []
-    for c0, c1 in ((0, 8), (8, 40), (40, 72)):
-        a_m.append(done("a", S.activation(T.msk[:, 16 * c0:16 * c1], T.mt[:].indirect(T.clsu[:, c0:c1]), COPY)))
-    wait("a", m_tr)
-    a_tr = done("a", S.activation(T.trb[:], ptr[:, 0:256], COPY))
+    def mask(c0, c1):
+        return done("a", S.activation(T.msk[:, 16 * c0:16 * c1], T.mt[:].indirect(T.clsu[:, c0:c1]), COPY))
 
-    def children(k, c0, c1):
-        wait("v", a_m[k])
+    def children(c0, c1, masked):
+        wait("v", masked)
         return done("v", V.tensor_tensor(T.l1[:, 16 * c0:16 * c1], T.kt[:].indirect(T.colu[:, c0:c1]),
                                          T.msk[:, 16 * c0:16 * c1], A.mult))
 
@@ -187,27 +154,26 @@ def rank_program(g, core, T, topo):
             ins = PE.matmul(out, T.sel[:, o:o + 128], T.l1[:, c0 + r:c1:4], r == 0, r == 3)
         return done("p", ins)
 
+    wait("a", c_cls)
+    a_m = [mask(0, 16), mask(16, 44), mask(44, 72)]
+    wait("a", m_tr)
+    a_tr = done("a", S.activation(T.trb[:], ptr[:, 0:256], COPY))
+
     wait("v", c_col, ("lkid", 16), i_k)
-    v_g = children(0, 0, 8)
-    v_n0 = children(1, 8, 40)
-    wait("p", v_g, c_sel0, c_sel1)
-    m_g = [to_lists(pg[X][:, 0:32], X, 0, 128) for X in range(2)]
-    c_goff = []
-    for X in range(2):
-        wait("v", m_g[X])
+    v_n0 = children(0, 16, a_m[0])
+    children(16, 44, a_m[1])
+    v_n1 = children(44, 72, a_m[2])
+    wait("p", c_sel0, c_sel1, v_n0)
+    first = [to_lists(pg[X][:, 0:64], X, 0, 256) for X in range(2)]
+    wait("p", v_n1)
+    m_n = [(first[X], to_lists(pn[X][:, 0:224], X, 256, 1152)) for X in range(2)]
+
+    def given(X):
+        wait("v", m_n[X][0])
         x = done("v", V.tensor_scalar(T.gx[:, 32 * X:32 * X + 32], pg[X][:, 0:32], f_c, 0.0, A.add, A.max))
         wait("v", x)
-        c_goff.append(done("v", V.tensor_scalar(T.goff[:, 32 * X:32 * X + 32], T.gx[:, 32 * X:32 * X + 32],
-                                                float(Z1), None, A.min)))
-    done("v", V.tensor_scalar(T.dmb[:, 0:KV], T.r1[:, 0:KV], f_k, None, A.is_equal))
-    c_dm = done("v", V.tensor_scalar(T.dmf[:, KV:32], T.r1[:, KV:32], f_k, None, A.is_equal))
-    v_n1 = children(2, 40, 72)
-    m_n = []
-    for X in range(2):
-        wait("p", v_n0)
-        to_lists(pn[X][:, 0:128], X, 128, 640)
-        wait("p", v_n1)
-        m_n.append(to_lists(pn[X][:, 128:256], X, 640, 1152))
+        return done("v", V.tensor_scalar(T.goff[:, 32 * X:32 * X + 32], T.gx[:, 32 * X:32 * X + 32],
+                                         float(Z1), None, A.min))
 
     def gather(q, out, window, offs):
         if q == "v":
@@ -216,13 +182,9 @@ def rank_program(g, core, T, topo):
 
     peers = [T.cores[(rank + d) % N] for d in range(1, N)]
 
-    def give_away(X):
-        got = []
-        for k, q in enumerate("va"):
-            wait(q, c_goff[X], LEX[X])
-            o, c = 512 * X + 256 * k, 32 * X + 16 * k
-            got.append(gather(q, T.gs[:, o:o + 256], win[X][:, 0:G0], T.goff[:, c:c + 16]))
-        wait("g", *got)
+    def give_away(X, lists):
+        wait("a", lists, LEX[X])
+        wait("g", gather("a", T.gs[:, 512 * X:512 * X + 512], win[X][:, 0:G0], T.goff[:, 32 * X:32 * X + 32]))
         moves = []
         for k, peer in enumerate(peers):
             eng = topo.engines(core, peer)
@@ -238,29 +200,39 @@ def rank_program(g, core, T, topo):
     arrive = sum(len(topo.engines(peer, core)) // len(peers) for peer in peers)
 
     def offsets(X):
-        k, u = pn[X][:, 0:256], T.nx[:, 256 * X:256 * X + 256]
-        wait("v", m_n[X])
-        x = done("v", V.tensor_scalar(u, k, f_a1, f_a2, A.subtract, A.max))
-        wait("v", x)
-        x = done("v", V.tensor_tensor(u, u, k, A.min))
-        wait("v", x)
-        return done("v", V.tensor_scalar(T.noff[:, 256 * X:256 * X + 256], u, f_c, 0.0, A.add, A.max))
-
-    def weights_v(k0, k1):
-        for k in range(k0, k1):
-            x = done("v", V.tensor_scalar(T.wt[:, 256 * k:256 * k + 256], T.trb[:], T.dmb[:, k:k + 1], None, A.mult))
+        parts = []
+        for o, w, k in ((256 * X, 32, pg[X][:, 32:64]), (256 * X + 32, 224, pn[X][:, 0:224])):
+            parts.append((k, T.nx[:, o:o + w], T.noff[:, o:o + w]))
+        wait("v", *m_n[X])
+        xs = [done("v", V.tensor_scalar(u, k, f_a1, f_a2, A.subtract, A.max)) for k, u, o in parts]
+        ys = []
+        for x, (k, u, o) in zip(xs, parts):
+            wait("v", x)
+            ys.append(done("v", V.tensor_tensor(u, u, k, A.min)))
+        for y, (k, u, o) in zip(ys, parts):
+            wait("v", y)
+            x = done("v", V.tensor_scalar(o, u, f_c, 0.0, A.add, A.max))
         return x
 
-    give_away(0)
-    wait("v", a_tr, c_dm)
-    wait("a", a_tr, c_dm)
-    weights_v(0, 12)
+    def weights(q, k0, k1):
+        wait(q, a_tr, c_dm)
+        for k in range(k0, k1):
+            o = T.wt[:, 256 * k:256 * k + 256]
+            if q == "v":
+                x = done("v", V.tensor_scalar(o, T.trb[:], T.dmb[:, k:k + 1], None, A.mult))
+            else:
+                x = done("a", S.activation(o, T.trb[:], IDENT, scale=T.dmf[:, k:k + 1]))
+        return x
+
+    c_g0 = given(0)
+    weights("a", KV, KV + 2)
+    give_away(0, c_g0)
+    c_g1 = given(1)
+    weights("v", 0, 8)
     c_noff = [offsets(0)]
-    w_v = weights_v(12, KV)
-    for k in range(KV, 32):
-        w_a = done("a", S.activation(T.wt[:, 256 * k:256 * k + 256], T.trb[:], IDENT, scale=T.dmf[:, k:k + 1]))
-    give_away(1)
-    c_noff.append(offsets(1))
+    w_v = weights("v", 8, KV)
+    w_a = weights("a", KV + 2, 32)
+    give_away(1, c_g1)
 
     wait("p", w_v, w_a)
     last = {}
@@ -282,12 +254,14 @@ def rank_program(g, core, T, topo):
 
     for X in range(2):
         for d in range(8):
+            if X == 0 and d == 3:
+                c_noff.append(offsets(1))
             got = []
-            for k, q in enumerate("va"):
-                wait(q, c_noff[X], ("arr%d" % X, arrive))
+            for k, q in enumerate(SHARE[X][d]):
+                wait(q, c_noff[X], LEX[X], ("arr%d" % X, arrive))
                 o, c = 4096 * X + 512 * d + 256 * k, 256 * X + 32 * d + 16 * k
                 got.append(gather(q, T.vv[:, o:o + 256], win[X][:], T.noff[:, c:c + 16]))
-            if X == 1 and d == 0:
+            if X == 1 and d == 2:
                 put_out(0)
             wait("p", *got)
             for Q in range(2):

from concourse.bass import DstId, RemoteDMATransfer
from concourse.mybir import AluOpType, ActivationFunctionType

N, P, E, M, G = 5, 3072, 8192, 128, 32
DX, DY = (-1, 0, 1, -1, 1, -1, 0, 1), (-1, -1, -1, 0, 0, 1, 1, 1)
HALF = E // 2
D0 = 16
Z1 = D0 + HALF
G0 = Z1 + 16
WW = G0 + 4 * G * (N - 1)
KQ = P // 4
KV = 23
SHARE = (("va", "va", "va", "aa", "va", "va", "va", "va"), ("va",) * 8)
B, F, I, U = "bfloat16", "float32", "int32", "uint16"
SCRATCH = {n: ("sbuf", [128, w], t) for n, w, t in (
    ("win0", WW, B), ("win1", WW, B), ("kt", KQ + 136, I), ("ng", 72, I), ("t1", 72, I), ("t2", 72, I),
    ("t3", 72, I), ("clsu", 72, U), ("colu", 72, U), ("trs", 108, B), ("trb", 256, B), ("pi", 8, I), ("pf", 16, F),
    ("r1", 128, F), ("prm", 256, B), ("sel", 1024, F), ("mt", 8, F), ("dmb", 32, B), ("dmf", 32, F),
    ("msk", 1152, F), ("l1", 1152, F), ("gx", 64, F), ("goff", 64, U), ("nx", 512, F), ("noff", 512, U),
    ("wt", 8192, B), ("gs", 1024, B), ("vv", 8192, B), ("ys", 512, F))}
SCRATCH.update({n: ("psum", [128, 512], F) for n in ("pg0", "pg1", "pn0", "pn1", "py0", "py1", "py2", "py3")})
SEMAPHORES = ["sv", "sa", "sp", "sg", "lng", "ltr", "lkid", "lex0", "lex1", "arr0", "arr1", "sent", "st0", "st1"]


def far_runs():
    runs = []
    for c in range(4):
        i = 0
        last = -2
        for ds in range(32):
            d, s = divmod(ds, 4)
            if max(abs(2 * DX[d] + s % 2 - c % 2), abs(2 * DY[d] + s // 2 - c // 2)) > 1:
                if ds == last + 1:
                    runs[-1][3] += 1
                else:
                    runs.append([c, ds, 27 * c + i, 1])
                last = ds
                i += 1
    return runs


def rank_program(g, core, T, topo):
    rank = T.rank_of(core)
    if rank is None:
        return
    A = AluOpType
    COPY = ActivationFunctionType.Copy
    IDENT = ActivationFunctionType.Identity
    queue = {"v": g.vector, "a": g.scalar, "p": g.tensor, "g": g, "s": g.sync}
    counter = {"v": "sv", "a": "sa", "p": "sp", "g": "sg"}
    count = {"v": 0, "a": 0, "p": 0, "g": 0}
    seen = {}

    def wait(q, *deps):
        for name, val in deps:
            if seen.get((q, name), 0) < val:
                queue[q].wait_ge(T.sem[name], val)
                seen[(q, name)] = val

    def done(q, ins):
        ins.then_inc(T.sem[counter[q]], 1)
        count[q] += 1
        return (counter[q], count[q])

    V, S, PE = g.vector, g.scalar, g.tensor
    win = [T.win0, T.win1]
    pg, pn, py = [T.pg0, T.pg1], [T.pn0, T.pn1], [T.py0, T.py1, T.py2, T.py3]
    ptr = T.py3

    S.dma_start(T.ng[:, 0:8], T.give[:]).then_inc(T.sem.lng, 16)
    g.sync.dma_start(T.ng[:, 8:72], T.near[:]).then_inc(T.sem.lng, 16)
    S.dma_start(T.trs[:], T.tr[:]).then_inc(T.sem.ltr, 16)
    g.sync.dma_start(T.kt[:, 0:KQ], T.kid[:]).then_inc(T.sem.lkid, 16)
    for X in range(2):
        for Q in range(2):
            for h in range(2):
                p0, r0 = 64 * Q + 32 * h, 64 * X + 32 * Q
                g.sync.dma_start(win[X][p0:p0 + 32, D0:Z1],
                                 T.ex[r0:r0 + 32, HALF * h:HALF * (h + 1)]).then_inc(T.sem["lex%d" % X], 16)
    LEX = [("lex0", 64), ("lex1", 64)]

    i_p = done("g", g.iota(T.pi[:, 0:1], [[0, 1]], 0, 1))
    i_r = done("g", g.iota(T.r1[:], [[32, 2], [0, 2], [1, 32]], 0, 0, allow_small_or_imprecise_dtypes=True))
    i_k = done("g", g.iota(T.kt[:, KQ:KQ + 128], [[4, 128]], E + 20, 0))

    done("v", V.memset(ptr[:, 0:256], 0.0))
    done("v", V.memset(T.kt[:, KQ + 128:KQ + 136], E))
    for X in range(2):
        done("v", V.memset(win[X][:, 0:D0], 0.0))
        done("v", V.memset(win[X][:, Z1:G0], 0.0))
    wait("v", i_p)
    p = T.pi[:, 0:1]
    done("v", V.tensor_scalar(T.pi[:, 1:2], p, 31, None, A.bitwise_and))
    done("v", V.tensor_scalar(T.pi[:, 2:3], p, 3, None, A.bitwise_and))
    done("v", V.tensor_scalar(T.pi[:, 3:4], p, 112, None, A.bitwise_and))
    done("v", V.tensor_scalar(T.pi[:, 4:5], p, 2, 3, A.arith_shift_right, A.bitwise_and))
    x = done("v", V.tensor_scalar(T.pi[:, 5:6], p, 5, 1, A.arith_shift_right, A.bitwise_and))
    wait("v", x)
    x = done("v", V.tensor_copy(T.pf[:, 0:6], T.pi[:, 0:6]))
    wait("v", x, i_r)
    f_p, f_k, f_lo, f_code, f_c, f_a1, f_a2 = (T.pf[:, j:j + 1] for j in (0, 1, 2, 6, 7, 8, 9))
    for X in range(2):
        c_perm = done("v", V.tensor_scalar(T.prm[:, 128 * X:128 * X + 128], T.r1[:], float(64 * X), f_p,
                                           A.add, A.is_equal))
    c_code = done("v", V.tensor_scalar(f_code, T.pf[:, 3:4], T.pf[:, 4:5], None, A.add))
    c_c = done("v", V.tensor_scalar(f_c, T.pf[:, 5:6], float(-HALF), float(D0), A.mult, A.add))
    done("v", V.tensor_scalar(f_a2, T.pf[:, 5:6], float(HALF), float(Z1 - D0), A.mult, A.add))
    done("v", V.tensor_scalar(T.mt[:], T.r1[:, 0:8], f_lo, None, A.is_equal))
    done("v", V.tensor_scalar(T.dmb[:, 0:KV], T.r1[:, 0:KV], f_k, None, A.is_equal))
    c_dm = done("v", V.tensor_scalar(T.dmf[:, KV:32], T.r1[:, KV:32], f_k, None, A.is_equal))
    wait("v", c_code, c_c)
    done("v", V.tensor_scalar(f_a1, f_c, float(E + 20 - G0), f_lo, A.add, A.subtract))

    def make_sel(X):
        for r in range(4):
            o = 128 * (4 * X + r)
            x = done("v", V.tensor_scalar(T.sel[:, o:o + 128], T.r1[:], float(64 * X - 4 * r), f_code,
                                          A.add, A.is_equal))
        return x

    c_sel0 = make_sel(0)

    wait("p", c_perm, ("ltr", 16))
    for X in range(2):
        for c, ds, col, n in far_runs():
            o = 64 * c + 32 * X + ds
            m_tr = done("p", PE.matmul(ptr[:, o:o + n], T.prm[:, 128 * X:128 * X + 128],
                                       T.trs[:, col:col + n], True, True))

    wait("v", ("lng", 32))
    x = done("v", V.tensor_scalar(T.t1[:], T.ng[:], float(3 * KQ), 2731.0, A.min, A.mult))
    wait("v", x)
    x = done("v", V.tensor_scalar(T.t2[:], T.t1[:], 21, None, A.arith_shift_right))
    wait("v", x)
    c_cls = done("v", V.tensor_copy(T.clsu[:], T.t2[:]))
    x = done("v", V.tensor_scalar(T.t3[:], T.t2[:], float(-KQ), None, A.mult))
    wait("v", x)
    x = done("v", V.tensor_tensor(T.t1[:], T.t3[:], T.ng[:], A.add))
    wait("v", x)
    c_col = done("v", V.tensor_copy(T.colu[:], T.t1[:]))
    c_sel1 = make_sel(1)

    def mask(c0, c1):
        return done("a", S.activation(T.msk[:, 16 * c0:16 * c1], T.mt[:].indirect(T.clsu[:, c0:c1]), COPY))

    def children(c0, c1, masked):
        wait("v", masked)
        return done("v", V.tensor_tensor(T.l1[:, 16 * c0:16 * c1], T.kt[:].indirect(T.colu[:, c0:c1]),
                                         T.msk[:, 16 * c0:16 * c1], A.mult))

    def to_lists(out, X, c0, c1):
        for r in range(4):
            o = 128 * (4 * X + r)
            ins = PE.matmul(out, T.sel[:, o:o + 128], T.l1[:, c0 + r:c1:4], r == 0, r == 3)
        return done("p", ins)

    wait("a", c_cls)
    a_m = [mask(0, 16), mask(16, 44), mask(44, 72)]
    wait("a", m_tr)
    a_tr = done("a", S.activation(T.trb[:], ptr[:, 0:256], COPY))

    wait("v", c_col, ("lkid", 16), i_k)
    v_n0 = children(0, 16, a_m[0])
    children(16, 44, a_m[1])
    v_n1 = children(44, 72, a_m[2])
    wait("p", c_sel0, c_sel1, v_n0)
    first = [to_lists(pg[X][:, 0:64], X, 0, 256) for X in range(2)]
    wait("p", v_n1)
    m_n = [(first[X], to_lists(pn[X][:, 0:224], X, 256, 1152)) for X in range(2)]

    def given(X):
        wait("v", m_n[X][0])
        x = done("v", V.tensor_scalar(T.gx[:, 32 * X:32 * X + 32], pg[X][:, 0:32], f_c, 0.0, A.add, A.max))
        wait("v", x)
        return done("v", V.tensor_scalar(T.goff[:, 32 * X:32 * X + 32], T.gx[:, 32 * X:32 * X + 32],
                                         float(Z1), None, A.min))

    def gather(q, out, window, offs):
        if q == "v":
            return done("v", V.tensor_copy(out, window.indirect(offs)))
        return done("a", S.activation(out, window.indirect(offs), COPY))

    peers = [T.cores[(rank + d) % N] for d in range(1, N)]

    def give_away(X, lists):
        wait("a", lists, LEX[X])
        wait("g", gather("a", T.gs[:, 512 * X:512 * X + 512], win[X][:, 0:G0], T.goff[:, 32 * X:32 * X + 32]))
        moves = []
        for k, peer in enumerate(peers):
            eng = topo.engines(core, peer)
            per = len(eng) // len(peers)
            rid, pid = topo.addr(peer)[:2]
            moves.append(RemoteDMATransfer(
                dst_ids=[DstId(rid=rid, pnc=pid)], dma_engine_mask=sum(1 << e for e in eng[per * k:per * (k + 1)]),
                remote_sem=T.sem["arr%d" % X], src=T.gs[:, 512 * X + 128 * k:512 * X + 128 * (k + 1)],
                dst=win[X][:, G0 + 128 * k:G0 + 128 * (k + 1)]))
        g.remote_dma_fused(moves, local_sem=T.sem.sent)

    sent = sum(len(topo.engines(core, peer)) // len(peers) for peer in peers)
    arrive = sum(len(topo.engines(peer, core)) // len(peers) for peer in peers)

    def offsets(X):
        parts = []
        for o, w, k in ((256 * X, 32, pg[X][:, 32:64]), (256 * X + 32, 224, pn[X][:, 0:224])):
            parts.append((k, T.nx[:, o:o + w], T.noff[:, o:o + w]))
        wait("v", *m_n[X])
        xs = [done("v", V.tensor_scalar(u, k, f_a1, f_a2, A.subtract, A.max)) for k, u, o in parts]
        ys = []
        for x, (k, u, o) in zip(xs, parts):
            wait("v", x)
            ys.append(done("v", V.tensor_tensor(u, u, k, A.min)))
        for y, (k, u, o) in zip(ys, parts):
            wait("v", y)
            x = done("v", V.tensor_scalar(o, u, f_c, 0.0, A.add, A.max))
        return x

    def weights(q, k0, k1):
        wait(q, a_tr, c_dm)
        for k in range(k0, k1):
            o = T.wt[:, 256 * k:256 * k + 256]
            if q == "v":
                x = done("v", V.tensor_scalar(o, T.trb[:], T.dmb[:, k:k + 1], None, A.mult))
            else:
                x = done("a", S.activation(o, T.trb[:], IDENT, scale=T.dmf[:, k:k + 1]))
        return x

    c_g0 = given(0)
    weights("a", KV, KV + 2)
    give_away(0, c_g0)
    c_g1 = given(1)
    weights("v", 0, 8)
    c_noff = [offsets(0)]
    w_v = weights("v", 8, KV)
    w_a = weights("a", KV + 2, 32)
    give_away(1, c_g1)

    wait("p", w_v, w_a)
    last = {}

    def put_out(X):
        e = []
        for Q, q in enumerate("va"):
            o = 256 * X + 128 * Q
            wait(q, last[(X, Q)])
            if q == "v":
                e.append(done("v", V.tensor_copy(T.ys[:, o:o + 128], py[2 * X + Q][:, 0:128])))
            else:
                e.append(done("a", S.activation(T.ys[:, o:o + 128], py[2 * X + Q][:, 0:128], COPY)))
        for Q in range(2):
            o, r0 = 256 * X + 128 * Q, 64 * X + 32 * Q
            q, sem = ("a", T.sem.st1) if (X, Q) == (1, 1) else ("s", T.sem.st0)
            wait(q, e[Q])
            queue[q].dma_start(T.y[r0:r0 + 32, :], T.ys[:, o:o + 128]).then_inc(sem, 16)

    for X in range(2):
        for d in range(8):
            if X == 0 and d == 3:
                c_noff.append(offsets(1))
            got = []
            for k, q in enumerate(SHARE[X][d]):
                wait(q, c_noff[X], LEX[X], ("arr%d" % X, arrive))
                o, c = 4096 * X + 512 * d + 256 * k, 256 * X + 32 * d + 16 * k
                got.append(gather(q, T.vv[:, o:o + 256], win[X][:], T.noff[:, c:c + 16]))
            if X == 1 and d == 2:
                put_out(0)
            wait("p", *got)
            for Q in range(2):
                for s in range(4):
                    o = 4096 * X + 512 * d
                    ins = PE.matmul(py[2 * X + Q][:, 0:128], T.wt[64 * Q:64 * Q + 64, 32 * X + 4 * d + s:8192:64],
                                    T.vv[64 * Q:64 * Q + 64, o + s:o + 512:4], d == 0 and s == 0, d == 7 and s == 3)
                if d == 7:
                    last[(X, Q)] = done("p", ins)
    put_out(1)
    wait("s", ("st0", 48))
    wait("a", ("st1", 16))
    wait("g", ("sent", 2 * sent))
